import numpy as np, ml_dtypes
CORES = [25,29,65,69,153,157,193,197]
N = 8
BF = ml_dtypes.bfloat16
def gentries(a):
    return np.ascontiguousarray(a.reshape(8, 16, -1).transpose(0, 2, 1)).reshape(8, -1)
def gtable(e):
    e = np.asarray(e); return np.ascontiguousarray(e.reshape(8, -1, 16).transpose(0, 2, 1)).reshape(128, -1).astype(np.int32)
PN, NT, ND, L, V, ST, H = 4096, 512, 512, 128, 3, 4, 1
def parts(rng):
    prog = rng.integers(0, 16, (N, 8, 16, PN)); eff = rng.integers(0, 16, (N, 8, 16, ND)); x = rng.integers(0, 16, (N, 8, 16, L)); goal = rng.integers(0, 16, (N, 8, 16, L))
    wt = rng.integers(0, 256, (N, 8, 16)); team = rng.integers(0, PN, (N, 8, 16, NT)); start = rng.integers(0, NT, (N, 8, L))
    hub = rng.integers(0, NT, (8, 12)); gi = np.arange(8)[None, :, None]; u = rng.random((N, 8, PN))
    act = np.where(u < 0.4, rng.integers(0, NT, u.shape), np.where(u < 0.65, hub[gi, rng.integers(0, 12, u.shape)], NT + rng.integers(0, ND, u.shape)))
    start = np.where(rng.random(start.shape) < 0.3, hub[gi, rng.integers(0, 12, start.shape)], start)
    return [prog, act, team, eff, x, goal, wt, start]
def pack(p):
    prog, act, team, eff, x, goal, wt, start = p
    def b(a): return np.ascontiguousarray(a.reshape(N, 128, -1)).astype(np.float32).astype(BF)
    def i(a): return np.ascontiguousarray(a.reshape(N, 128, -1)).astype(np.int32)
    return {"prog": b(prog), "act": np.ascontiguousarray(act).astype(np.int32), "team": i(team), "eff": b(eff), "x0": b(x), "goal": b(goal), "wt": i(wt), "start": np.stack([gtable(a) for a in start])}
def setup_inputs(rng):
    p = parts(rng); prog, act, team, eff, x, goal, wt, start = p
    for q in range(N):
        for g in range(8):
            t = rng.permutation(NT)[:2]; j = rng.permutation(L)[:6]
            team[q, g][:, t] = 0; act[q, g, 0] = t[0]; start[q, g, j[:3]] = t[0]; start[q, g, j[3:]] = t[1]
    return pack(p)
def setup_inputs_corners(rng):
    p = parts(rng); prog, act, team, eff, x, goal, wt, start = p
    for q in range(N):
        for g in range(8):
            m = (g + q) % 8
            if m == 0: act[q, g] = rng.integers(0, NT, PN)
            elif m == 1: act[q, g] = NT + rng.integers(0, ND, PN); goal[q, g] = x[q, g]
            elif m == 2: act[q, g] = rng.choice(np.array([0, NT - 1]), PN); start[q, g] = rng.choice(np.array([0, NT - 1, 1, NT - 2]), L)
            elif m == 3:
                t = int(rng.choice(np.array([0, NT - 1, NT // 2]))); act[q, g] = t; start[q, g, ::2] = t
            elif m == 4:
                start[q, g] = NT - 1; team[q, g, :, NT - 1] = 0
                act[q, g] = np.where(rng.random(PN) < 0.5, rng.integers(1, 9, PN), NT + rng.integers(0, ND, PN)); act[q, g, 0] = 0
            elif m == 5:
                act[q, g] = NT + rng.integers(0, ND, PN); eff[q, g] = 7; goal[q, g] = np.abs(x[q, g] - 7); team[q, g] = rng.choice(np.array([0, 1, PN - 2, PN - 1]), (16, NT))
            elif m == 6: prog[q, g] = prog[q, g, :, :1].copy(); wt[q, g] = 255 * rng.integers(0, 2, 16)
            else: eff[q, g, :, ::2] = 0; wt[q, g] = 0; x[q, g, :, ::4] = 0; x[q, g, :, 1::4] = 15
    return pack(p)
def two(rng, hi, n):
    return hi * np.where(rng.random((N, 8, 1, n)) < 0.5, rng.integers(0, 2, (N, 8, 1, n)), rng.integers(0, 2, (N, 8, 16, n)))
def setup_inputs_ends(rng):
    prog = two(rng, 15, PN); eff = two(rng, 15, ND); x = two(rng, 15, L); goal = two(rng, 15, L); wt = 255 * rng.integers(0, 2, (N, 8, 16))
    team = np.where(rng.random((N, 8, 16, NT)) < 0.8, two(rng, PN - 1, NT), rng.integers(0, PN, (N, 8, 16, NT)))
    s = (N, 8, PN); far = np.where(rng.random(s) < 0.5, rng.choice(np.array([1, NT - 1, NT, NT + ND - 2]), s), rng.integers(0, NT + ND, s))
    act = np.where(rng.random(s) < 0.75, (NT + ND - 1) * rng.integers(0, 2, s), far)
    s = (N, 8, L); start = np.where(rng.random(s) < 0.8, (NT - 1) * rng.integers(0, 2, s), rng.integers(0, NT, s))
    a6 = act[:, 6]; a6[a6 == NT - 1] = NT
    start[:, 6] = np.where(rng.random((N, L)) < 0.75, 0, rng.integers(1, NT - 1, (N, L))); start[:, 6, L - 1] = NT - 1
    wt[:, 6] = 0; wt[:, 6, 1::2] = 255; wt[:, 6, 0] = 17; x[:, 6, ::2, L - 1] = 15; x[:, 6, 1::2, L - 1] = 0; goal[:, 6, :, L - 1] = x[:, 6, :, L - 1]
    team[:, 6, :, NT - 1] = PN - 1; act[:, 6, ((((PN - 1) * 511) >> 5) + PN - 1) & (PN - 1)] = NT + ND - 1; eff[:, 6, :, ND - 1] = 15
    c = np.arange(PN); c = int(np.flatnonzero((((c >> 5) + c) & (PN - 1)) == PN - 1)[0])
    wt[:, 7] = 255; prog[:, 7, :, 0] = 15; prog[:, 7, :, PN - 1] = 15; team[:, 7, :, NT - 1] = 0; team[:, 7, 0, NT - 1] = c
    act[:, 7, PN - 1] = NT + ND - 1; act[:, 7, 0] = NT; eff[:, 7, :, ND - 1] = 15; eff[:, 7, :, 0] = 0
    x[:, 7, :, L - 1] = 0; goal[:, 7, :, L - 1] = 15; x[:, 7, :, L - 2] = 0; goal[:, 7, :, L - 2] = 0; x[:, 7, :, 0] = 15; goal[:, 7, :, 0] = 0
    start[:, 7, L - 2:] = NT - 1; start[:, 7, 0] = NT - 1
    x[:, 5, :, L - 1] = 0; goal[:, 5] = x[:, 5]; goal[:, 5, :, L - 1] = 15; start[:, 5, L - 1] = NT // 2
    team[:, 5, :, NT // 2] = c; team[:, 5, :, 0] = 0; team[:, 5, :, NT - 1] = PN - 1
    act[:, 5, PN - 1] = 0; act[:, 5, 0] = NT - 1; act[:, 5, (((PN - 1) >> 5) + PN - 1) & (PN - 1)] = NT + ND - 1; eff[:, 5, :, ND - 1] = 15
    return pack([prog, act, team, eff, x, goal, wt, start])
def setup_inputs_full(rng):
    p = parts(rng); prog, act, team, eff, x, goal, wt, start = p
    keys = np.array([3, 7, 11, 15]); c = np.arange(PN)
    same = np.stack([np.flatnonzero(((13 * c + 97 * int(e) + 1) & (PN - 1)) == c)[:4] for e in keys])
    for q in range(N):
        for g in range(8):
            m = (0, 1, 2, 3, 4, 1, 3, 0)[g]; S = rng.permutation(NT); o = rng.permutation(PN - PN // 16); n = o + (o >> 5)
            if m == 0:
                act[q, g] = NT + rng.integers(0, ND, PN); start[q, g] = S[:L]; eff[q, g] = 0; eff[q, g, :8] = 2
                x[q, g, :8] = rng.integers(2 * V, 16, (8, L)); near = np.argsort(rng.random((8, L)), axis=0) < rng.permutation(np.arange(L) % 5)[None, :]
                goal[q, g, :8] = x[q, g, :8] - 2 * V + 2 * near; goal[q, g, :8, int(rng.integers(0, L))] = 15
            elif m == 1:
                wt[q, g] = 0; start[q, g] = S[:L]; x[q, g] = rng.integers(8, 16, (16, L)); goal[q, g] = 0; eff[q, g] = rng.integers(0, 8, (16, ND)); eff[q, g, 0] = np.maximum(eff[q, g, 0], 1)
                act[q, g, n[:4 * L]] = S[L + rng.integers(0, L, 4 * L)]; act[q, g, n[4 * L:8 * L]] = S[2 * L + rng.integers(0, L, 4 * L)]; act[q, g, n[8 * L:12 * L]] = NT + rng.integers(0, ND, 4 * L)
                team[q, g][:, S[:L]] = o[:4 * L].reshape(4, L)[rng.integers(0, 4, (16, L)), np.arange(L)[None, :]]
                team[q, g][:, S[L:2 * L]] = o[4 * L + rng.integers(0, 4 * L, (16, L))]; team[q, g][:, S[2 * L:3 * L]] = o[8 * L + rng.integers(0, 4 * L, (16, L))]
            elif m == 2:
                act[q, g] = NT + rng.integers(0, ND, PN); start[q, g] = S[:L]; goal[q, g] = x[q, g]; eff[q, g] = np.maximum(eff[q, g], 1)
            elif m == 3:
                h = L // 4; j = rng.permutation(L); a, b = j[:h], j[h:2 * h]; ab = j[:2 * h]
                start[q, g] = S[rng.integers(2 * h, NT, L)]; start[q, g, ab] = S[:2 * h]; x[q, g][:, ab] = 0; goal[q, g][:, ab] = 15
                d = rng.permutation(ND)[:2]; eff[q, g, :, d[0]] = 15; eff[q, g, :, d[1]] = 0; eff[q, g, int(rng.integers(0, 16)), d[1]] = 1
                prog[q, g, :, n[0]] = 15; prog[q, g, :, n[1]] = 15; prog[q, g, int(rng.integers(0, 16)), n[1]] = 14; prog[q, g][:, n[2:2 + h]] = 0
                act[q, g, n[0]] = NT + d[0]; act[q, g, n[1]] = NT + d[1]; act[q, g, n[2:2 + h]] = S[h:2 * h]
                team[q, g][:, S[:2 * h]] = o[0]; team[q, g][rng.integers(1, 16, h), S[:h]] = o[1]
                team[q, g][rng.integers(0, 16, h) * rng.permutation(np.arange(h) % 2), S[h:2 * h]] = o[2:2 + h]
            else:
                h = L // 2; j = np.sort(rng.permutation(L).reshape(h, 2), axis=1); w = rng.integers(0, 4, h)
                wt[q, g] = 0; wt[q, g, 0] = 1; act[q, g] = NT + rng.integers(0, ND, PN); eff[q, g] = np.maximum(eff[q, g], 1); eff[q, g, 0] = 0
                x[q, g, 0, j[:, 0]] = keys[w]; x[q, g, 0, j[:, 1]] = 2 * rng.integers(0, 8, h); goal[q, g] = x[q, g]
                start[q, g, j[:, 0]] = S[:h]; start[q, g, j[:, 1]] = S[:h]; team[q, g][:, S[:h]] = same[w[None, :], rng.integers(0, same.shape[1], (16, h))]
    return pack(p)
def setup_inputs_spread(rng):
    def v(n): return rng.integers(0, 16, (N, 8, 16, n)) >> rng.integers(0, 4, (N, 8, 1, n))
    def w(n, shape):
        k = rng.choice(np.array([0.5, 1.0, 2.0, 3.0]), (N, 8) + (1,) * (len(shape) - 2)); return np.minimum((n * rng.random(shape) ** k).astype(np.int64), n - 1)
    return pack([v(PN), w(NT + ND, (N, 8, PN)), w(PN, (N, 8, 16, NT)), v(ND), v(L), v(L), w(256, (N, 8, 16)), w(NT, (N, 8, L))])
def setup_inputs_ties(rng):
    p = parts(rng); prog, act, team, eff, x, goal, wt, start = p
    pat = rng.integers(0, 3, (N, 8, 16, 32)); prog = np.take_along_axis(pat, rng.integers(0, 32, (N, 8, 1, PN)), 3)
    eff = rng.integers(0, 3, eff.shape); x = rng.integers(0, 3, x.shape); goal = rng.integers(0, 3, goal.shape)
    team[:, :, 8:, ::2] = team[:, :, :8, ::2]
    return pack([prog, act, team, eff, x, goal, wt, start])
def check_inputs(d):
    bad = []
    for k, lo, hi in (("prog", 0, 15), ("act", 0, NT + ND - 1), ("team", 0, PN - 1), ("eff", 0, 15), ("x0", 0, 15), ("goal", 0, 15), ("wt", 0, 255), ("start", 0, NT - 1)):
        a = np.asarray(d[k]).astype(np.float64)
        if not (np.min(a) >= lo and np.max(a) <= hi): bad.append("range of " + k)
        elif np.any(a != np.floor(a)): bad.append("whole numbers in " + k)
    return bad
def nums(a, n):
    return a.astype(np.float32).astype(np.int32).reshape(N, 8, 16, n)
def reference(prog, act, team, eff, x0, goal, wt, start):
    P = nums(prog, PN); D = nums(eff, ND); x = nums(x0, L); z = nums(goal, L); w = nums(wt, 1)
    T = team.astype(np.int64).reshape(N, 8, 16, NT); a = act.astype(np.int64)
    s = np.stack([gentries(t) for t in start]).astype(np.int64); A = np.zeros((N, 8), np.int64)
    for v in range(V):
        nx = np.zeros_like(x); ns = np.zeros_like(s)
        for r in range(N):
            q = (r + H * v) % N; X = x[r]; Y = X; cur = s[r]; trail = [cur]
            e = np.add.reduce(w[q] * X, axis=1).astype(np.int64) & 255
            go = np.ones((8, L), bool); won = np.zeros((8, L), bool); lastk = np.zeros((8, L), np.int64); lastt = np.zeros((8, L), np.int64); first = lastk
            for i in range(ST):
                c = np.take_along_axis(T[q], cur[:, None, :], 2)
                n = (((c * (2 * e[:, None, :] + 1)) >> 5) + c) & (PN - 1)
                d = np.take_along_axis(P[q], n.reshape(8, 1, 16 * L), 2).reshape(8, 16, 16, L) - X[:, :, None, :]
                score = np.add.reduce(np.abs(d), axis=1)
                ak = np.take_along_axis(a[q], n.reshape(8, 16 * L), 1).reshape(8, 16, L)
                bar = np.zeros((8, 16, L), bool)
                for t in trail: bar = bar | (ak == t[:, None, :])
                k = np.argmin(np.where(bar, 1000000, score), axis=1)
                ok = go & ~np.all(bar, axis=1)
                an = np.take_along_axis(ak, k[:, None, :], 1)[:, 0]
                if i == 0: first = np.take_along_axis(n, k[:, None, :], 1)[:, 0]
                lastk = np.where(ok, k, lastk); lastt = np.where(ok, cur, lastt); won = won | ok
                fin = ok & (an >= NT); j = np.where(fin, an - NT, 0)
                Y = np.where(fin[:, None, :], np.abs(X - np.take_along_axis(D[q], j[:, None, :], 2)), Y)
                go = ok & ~fin; cur = np.where(go, an, cur); trail.append(cur)
            old = np.add.reduce(np.abs(X - z[r]), axis=1); new = np.add.reduce(np.abs(Y - z[r]), axis=1)
            good = new < old - (A[q] & 7)[:, None]
            up = good & (cur != s[r]); fail = won & ~good
            for g in range(8):
                j = np.flatnonzero(up[g]); u, ix = np.unique(first[g, j], return_index=True); a[q, g, u] = cur[g, j[ix]]
                j = np.flatnonzero(fail[g]); u, ix = np.unique(lastt[g, j], return_index=True); j = j[ix]; k = lastk[g, j]
                T[q, g, k, u] = (13 * T[q, g, k, u] + 97 * e[g, j] + 1) & (PN - 1)
            A[q] = A[q] + np.add.reduce(good.astype(np.int64), axis=1)
            nx[r] = Y; ns[r] = cur
        x, s = nx, ns
    return {"yteam": T.reshape(N, 128, NT).astype(np.float32), "yact": a.astype(np.float32), "yx": x.reshape(N, 128, L).astype(np.float32).astype(BF)}

from concourse.mybir import AluOpType, AxisListType, ActivationFunctionType

AL = AluOpType
AF = ActivationFunctionType
PN, NT, NV, ST = 4096, 512, 3, 4
RV = float(2 ** 24 - 1024)
BIG = float(2 ** 24)
KW = PN + NT + 128
CV = [0, 2, 5, 8, 11, 14, 16]
CS = [0, 2, 6, 10, 13, 15, 16]
SA = 8
NY = 2 * (16 - SA)
QE = "sssvsvsv"
DO = {3: 0, 4: 64, 5: 144, 6: 240, 7: 352, 8: 480}


def _tensor_order():
    def ends(ch, fixed):
        t, out = 0.0, {}
        for a0, a1 in zip(ch, ch[1:]):
            t += fixed + 166.0 * (a1 - a0)
            out.update({a: t for a in range(a0, a1)})
        return out
    ev, es = ends(CV, 50.0), ends(CS, 65.0)
    todo = [(k, a, (ev if k == 2 else es)[a]) for k in range(3) for a in range(16)]
    t, order = 0.0, []
    while todo:
        ready = [o for o in todo if o[2] <= t] or [min(todo, key=lambda o: o[2])]
        o = min(ready)
        todo.remove(o)
        order.append(o[:2])
        t = max(t, o[2]) + 56.0
    return order


def _names(p, a0, a1):
    return " ".join("%s%d" % (p, a) for a in range(a0, a1))


f32, bf, i32, u16 = "float32", "bfloat16", "int32", "uint16"


def _sb(n, d):
    return ("sbuf", [128, n], d)


SCRATCH = {
    "P": _sb(PN, bf), "Q": _sb(KW, bf), "TW": _sb(PN + 1032, f32), "AW": _sb(KW, f32), "EW": _sb(1040, bf),
    "M": _sb(2048, bf), "G": _sb(2048, bf), "XE": _sb(2048, bf), "Y4": _sb(16 * NY, bf),
    "X0": _sb(136, bf), "X1": _sb(136, bf), "X2": _sb(136, bf), "XF": _sb(128, bf),
    "O0": _sb(144, bf), "O1": _sb(144, bf), "O2": _sb(144, bf),
    "G0": _sb(128, bf), "G1": _sb(128, bf), "G2": _sb(128, bf),
    "ai": _sb(512, i32), "ai2": _sb(512, i32), "lh": _sb(512, bf), "ti": _sb(512, i32), "wi0": _sb(4, i32), "sti": _sb(8, i32),
    "sel": _sb(1024, bf), "sa": _sb(2048, bf), "Z": _sb(4 * 144, bf), "Y": _sb(128, bf),
    "ip": _sb(8, i32), "pf": _sb(16, f32), "ic": _sb(128, i32), "il": _sb(176, i32), "iy": _sb(16, i32),
    "cm": _sb(128, i32), "cdv": _sb(128, i32), "cb": _sb(128, bf),
    "MK": _sb(128, f32), "BO": _sb(128, bf), "BO32": _sb(128, f32), "ID": _sb(128, bf), "NI": _sb(128, bf), "BI": _sb(128, bf),
    "I32": _sb(128, f32), "I12": _sb(128, f32),
    "WB": _sb(128, bf), "KI": _sb(128, bf), "D0": _sb(128, f32), "DS": _sb(128, f32),
    "i8": _sb(8, f32), "lam": _sb(8, f32), "dum": _sb(8, f32), "cdm": _sb(8, f32), "dumf": _sb(8, f32),
    "LS": _sb(176, u16), "PL": _sb(8, u16), "YL": _sb(NY, u16),
    "e1": _sb(128, i32), "e2": _sb(128, i32), "E33": _sb(128, f32), "E97": _sb(128, f32),
    "m32": _sb(128, i32), "n0": _sb(128, i32), "n1": _sb(128, i32), "n16": _sb(128, u16),
    "TX": _sb(512, f32), "EQ": _sb(512, bf), "W": _sb(128, f32),
    "H": _sb(40, i32), "WI": _sb(40, i32), "lst": _sb(8, u16), "dl": _sb(8, f32), "D": _sb(8, f32),
    "ge": _sb(40, f32), "lt": _sb(40, f32), "vv": _sb(40, f32), "CU": _sb(40, f32),
    "dx": _sb(128, bf), "uo": _sb(128, bf), "un": _sb(128, bf),
    "k0": _sb(8, i32), "k0x": _sb(128, bf), "nf": _sb(128, f32), "fm": _sb(128, f32), "fs": _sb(128, f32), "fl": _sb(8, u16),
    "qk": _sb(128, f32), "qv": _sb(128, bf), "av": _sb(128, f32),
    "kk": _sb(40, i32), "a1": _sb(40, f32), "nv": _sb(40, f32), "va": _sb(40, f32),
    "vt": _sb(40, f32), "vk": _sb(40, f32), "LT": _sb(40, f32), "LK": _sb(40, f32), "tl": _sb(8, u16),
    "s8": _sb(16 * 8, f32), "hf": _sb(32, f32), "kx": _sb(128, f32),
    "c1": _sb(128, f32), "u1": _sb(128, f32), "u2": _sb(128, f32), "t3": _sb(128, i32), "tv": _sb(128, i32),
    "df": _sb(192, f32), "db": _sb(480, bf), "dr": _sb(480, bf), "dm": _sb(496, bf), "wl": _sb(2, u16), "wr": _sb(16, f32),
    "sl": _sb(8, u16), "cn": _sb(4, f32), "ac": _sb(8, i32), "thr": _sb(4, f32),
}
for _b in range(8):
    SCRATCH["B%d" % _b] = ("psum", [128, 512], f32)

NDMA = 28
SEMAPHORES = ["cv", "cs", "cp", "cg", "ls", "ag1", "ag2", "am1", "am2", "af", "r0", "r1", "r2", "r3"] + ["d%d" % _i for _i in range(NDMA)]


def _relay(T, topo, src):
    n = len(T.cores)
    far = T.cores[(T.rank_of(src) + 2) % n]
    best = [c for c in topo.cores_of(src) if T.rank_of(c) is None and topo.may_write(c, far)]
    near = [c for c in best if topo.die(c) == topo.die(src)]
    return (near or best)[0]


def _messages(T, rank):
    n = len(T.cores)
    return [("G0", 128, [((rank + 1) % n, "G1", "ag1"), ((rank + 2) % n, "G2", "ag2")]),
            ("O0", 136, [((rank + 1) % n, "X1", "am1")]),
            ("O1", 136, [((rank + 1) % n, "X2", "am2")]),
            ("O2", 128, [((rank - 2) % n, "XF", "af")])]


def _cnt(topo, a, b):
    return len(topo.engines(a, b))


def _relay_program(g, core, src, T, topo):
    total = 0
    for i, (buf, w, dsts) in enumerate(_messages(T, T.rank_of(src))):
        far = [d for d in dsts if not topo.may_write(src, T.cores[d[0]])]
        if not far:
            continue
        g.wait_ge(T.sem["r%d" % i], _cnt(topo, src, core))
        for r, land, sem in far:
            d = T.cores[r]
            rid, pid = topo.addr(d, core)
            g.remote_dma(T[land][:, 0:w], T[buf][:, 0:w], T.sem[sem], T.sem.ls, pid, rid, topo.mask(core, d))
            total += _cnt(topo, core, d)
    g.wait_ge(T.sem.ls, total)


def _emit(ops, g, T):
    qs = {"v": g.vector, "s": g.scalar, "p": g.tensor, "g": g, "y": g.sync}
    writer, readers, clock, pos, plan = {}, {}, {k: {} for k in qs}, {k: 0 for k in qs}, []
    for i, o in enumerate(ops):
        e = o["e"]
        deps = set()
        for r in o["r"]:
            if r in writer:
                deps.add(writer[r])
            if r[0] == "B" and r[1:].isdigit():
                deps.update(j for j in readers.get(r, []) if ops[j]["e"] != e)
        for w in o["w"]:
            if w in writer:
                deps.add(writer[w])
            deps.update(readers.get(w, []))
        waits = []
        if e is not None:
            ck = clock[e]
            for j in sorted(deps, reverse=True):
                d = ops[j]
                if e == "p" and d["e"] == "p":
                    continue
                if ck.get(d["src"], -1) >= d["pos"]:
                    continue
                waits.append(j)
                d["need"] = True
                for k, val in d["ck"].items():
                    if ck.get(k, -1) < val:
                        ck[k] = val
        if o["kind"] == "c":
            o["src"], o["pos"] = e, pos[e]
            pos[e] += 1
        else:
            o["src"], o["pos"] = i, 0
        o["ck"] = dict(clock[e]) if e is not None else {}
        o["ck"][o["src"]] = o["pos"]
        plan.append(waits)
        for r in o["r"]:
            readers.setdefault(r, []).append(i)
        for w in o["w"]:
            writer[w] = i
            readers[w] = []
    count, nd = {k: 0 for k in qs}, 0
    for i, o in enumerate(ops):
        if o["kind"] == "c" and o.get("need"):
            count[o["e"]] += 1
            o["sem"], o["val"] = T.sem["c" + o["e"]], count[o["e"]]
        elif o["kind"] == "d":
            o["sem"], o["val"] = T.sem["d%d" % nd], 16
            nd += 1
        if o["e"] is None:
            continue
        q = qs[o["e"]]
        for j in plan[i]:
            q.wait_ge(ops[j]["sem"], ops[j]["val"])
        if o["f"] is None:
            continue
        ins = o["f"](q)
        if o["kind"] == "d":
            ins.then_inc(o["sem"], 16)
        elif o["kind"] == "c" and o.get("need"):
            ins.then_inc(o["sem"], 1)


def rank_program(g, core, T, topo):
    rank = T.rank_of(core)
    if rank is None:
        for c in T.cores:
            if _relay(T, topo, c) == core:
                _relay_program(g, core, c, T, topo)
        return
    n = len(T.cores)
    ops = []
    sent = [0]

    def rec(e, kind, f, r, w, **kw):
        o = {"e": e, "kind": kind, "f": f, "r": r.split(), "w": w.split()}
        o.update(kw)
        ops.append(o)

    def dma(e, out, in_, r, w, **kw):
        rec(e, "d", lambda q: q.dma_start(out, in_, **kw), r, w)

    def ts(out, in0, s1, s2, o0, o1, r, w):
        if o1 is None:
            rec("v", "c", lambda q: q.tensor_scalar(out, in0, s1, None, o0), r, w)
        else:
            rec("v", "c", lambda q: q.tensor_scalar(out, in0, s1, s2, o0, o1), r, w)

    def tt(out, a, b, o, r, w):
        rec("v", "c", lambda q: q.tensor_tensor(out, a, b, o), r, w)

    def cp(out, in_, r, w):
        rec("v", "c", lambda q: q.tensor_copy(out, in_), r, w)

    def ms(ap, val, w):
        rec("v", "c", lambda q: q.memset(ap, val), "", w)

    def scan(out, a, b, o0, o1, r, w):
        rec("v", "c", lambda q: q.tensor_tensor_scan(out, a, b, 0.0, o0, o1), r, w)

    def red(out, in_, o, r, w, **kw):
        rec("v", "c", lambda q: q.tensor_reduce(out, in_, AxisListType.X, o, **kw), r, w)

    def act(out, in_, fn, r, w, **kw):
        rec("s", "c", lambda q: q.activation(out, in_, fn, **kw), r, w)

    def mm(out, lhsT, rhs, start, stop, r, w):
        rec("p", "c", lambda q: q.matmul(out, lhsT, rhs, start, stop), r, w)

    def iota(out, pat, base, cmul, w, **kw):
        rec("g", "c", lambda q: q.iota(out, pat, base, cmul, **kw), "", w)

    def send(i):
        buf, w, dsts = _messages(T, rank)[i]
        targets = [(T.cores[r], land, sem) for r, land, sem in dsts if topo.may_write(core, T.cores[r])]
        if len(targets) < len(dsts):
            targets.insert(0, (_relay(T, topo, core), buf, "r%d" % i))
        for d, land, sem in targets:
            rid, pid = topo.addr(d, core)
            sent[0] += _cnt(topo, core, d)
            rec("g", "x", lambda q, d=d, land=land, sem=sem, rid=rid, pid=pid: q.remote_dma(
                T[land][:, 0:w], T[buf][:, 0:w], T.sem[sem], T.sem.ls, pid, rid, topo.mask(core, d)),
                buf + (" " + buf + "c" if w > 128 else ""), "")

    def arrive(back, land, sem):
        src = T.cores[(rank - back) % n]
        last = src if topo.may_write(src, core) else _relay(T, topo, src)
        rec(None, "a", None, "", land, sem=T.sem[sem], val=_cnt(topo, last, core))

    arrive(1, "G1", "ag1"); arrive(2, "G2", "ag2"); arrive(1, "X1", "am1"); arrive(1, "X2", "am2"); arrive(-2, "XF", "af")
    direct = topo.may_write(T.cores[(rank - 1) % n], core)
    early = {1: direct, 2: not direct}

    K, A, GN, E, R1, R2, V1, V2 = [T["B%d" % b] for b in range(8)]
    pf, ip, ic, MK, H, WI, CU, s8 = T.pf, T.ip, T.ic, T.MK, T.H, T.WI, T.CU, T.s8
    TWIN = T.TW[:, PN:PN + 1032]
    TEAM = T.TW[:, PN:PN + NT]
    small = {"allow_small_or_imprecise_dtypes": True}

    def Zw(j, a):
        return T.Z[:, 144 * j + 15 - a:144 * j + 143 - a]

    def exl(s):
        return T.LS[:, 8 * s:8 * s + 8]

    def S8(j):
        return s8[:, 8 * j:8 * j + 8]

    dma("s", T.ai[0:64, :], T.act[:], "", "aia")
    dma("y", T.ai[64:128, :], T.act[:], "", "aib")
    dma("s", T.X0[:, 0:128], T.x0[:], "", "X0")
    dma("y", T.wi0[:, 0:1], T.wt[:], "", "wi0")
    for c in range(4):
        dma("s" if c % 2 == 0 else "y", T.P[:, 1024 * c:1024 * c + 1024], T.prog[:, 1024 * c:1024 * c + 1024], "", "P%d" % c)
        if c == 0:
            dma("y", T.ti[:], T.team[:], "", "ti")
            dma("y", T.sti[:], T.start[:], "", "sti")
    dma("y", T.G0[:], T.goal[:], "", "G0")
    dma("y", T.EW[:, 512:1024], T.eff[:], "", "EWb")
    PALL = "P0 P1 P2 P3"
    QALL = " ".join("Q%d" % c for c in range(8))

    iota(ip[:, 0:1], [[0, 1]], 0, 1, "ip0")
    iota(ic[:], [[1, 128]], 0, 0, "ic")
    iota(T.il[:, 48:176], [[1, 16], [16, 8]], 0, 0, "il2")
    iota(T.il[:, 0:40], [[1, 5], [5, 8]], 0, 0, "il0")
    iota(T.il[:, 40:48], [[1, 8]], 0, 0, "il1")
    iota(T.iy[:, 0:NY], [[1, NY // 2], [64, 2]], SA, 0, "iy")
    iota(T.KI[:], [[0, 8], [2048, 16]], 32768, 0, "KI", **small)
    send(0)
    iota(T.TW[:, PN + NT:PN + 1032], [[0, 520]], 0, 0, "TWz", **small)
    iota(T.EW[:, 0:512], [[0, 512]], 0, 0, "EWa", **small)
    iota(T.EW[:, 1024:1040], [[0, 16]], 0, 0, "EWc", **small)
    iota(H[:], [[0, 40]], 0, 0, "H1 H2 H3 H4 Hz")
    iota(WI[:], [[0, 40]], 0, 0, "WIz")
    iota(T.dr[:], [[0, 480]], 0, 0, "dr", **small)
    for b in range(3, 8):
        iota(T.dr[:, DO[b]:DO[b] + 1], [[0, 1]], 16384, 0, "dr", **small)
    ms(T.Z[:], 0.0, "Z")
    sh, an_ = AL.arith_shift_right, AL.bitwise_and
    mul, add, sub, eq = AL.mult, AL.add, AL.subtract, AL.is_equal
    p0 = ip[:, 0:1]
    ts(ip[:, 1:2], p0, 15, None, an_, None, "ip0", "ip1")
    ts(ip[:, 2:3], p0, 4, None, sh, None, "ip0", "ip2")
    ts(ip[:, 3:4], p0, 7, None, an_, None, "ip0", "ip3")
    ts(ip[:, 4:5], p0, 3, 1, sh, an_, "ip0", "ip4")
    ts(ip[:, 5:6], p0, 2, 3, sh, an_, "ip0", "ip5")
    ts(ip[:, 6:7], p0, 3, 7, sh, an_, "ip0", "ip6")
    ts(ip[:, 7:8], p0, 6, None, sh, None, "ip0", "ip7")
    cp(T.cb[:], ic[:], "ic", "cb")
    cp(pf[:, 0:8], ip[:], "ip0 ip1 ip2 ip3 ip4 ip5 ip6 ip7", "pf")
    pp, pm, pg = pf[:, 0:1], pf[:, 1:2], pf[:, 2:3]
    ts(T.cdv[:], ic[:], 4, None, sh, None, "ic", "cdv")
    ts(pf[:, 10:11], pf[:, 6:7], 16.0, pf[:, 7:8], mul, add, "pf", "pf10")
    ts(T.i8[:], ic[:, 0:8], pf[:, 3:4], None, eq, None, "ic pf", "i8")
    ts(T.Z[:, 15:143:16], ic[:, 0:8], pg, 65536.0, eq, mul, "ic pf Z", "Z0")
    ts(T.Y[:], T.cb[:], -1.0, pf[:, 10:11], add, eq, "cb pf10", "Y")
    for c in range(8):
        act(T.sel[:, 128 * c:128 * c + 128], T.Y[:], AF.Copy, "Y i8", "sel%d" % c, scale=T.i8[:, c:c + 1])
    cp(T.LS[:], T.il[:], "il0 il1 il2", "LS")
    ts(T.BO[:], T.cdv[:], pg, None, eq, None, "cdv pf", "BO")
    ts(T.cm[:], ic[:], 15, None, an_, None, "ic", "cm")
    ts(pf[:, 8:9], pf[:, 3:4], 16.0, pf[:, 4:5], mul, add, "pf", "pf8")
    ts(pf[:, 9:10], pf[:, 5:6], 16.0, None, mul, None, "pf", "pf9")
    ts(MK[:], T.cm[:], pm, None, eq, None, "cm pf", "MK")
    ts(T.ID[:], T.cb[:], pp, None, eq, None, "cb pf", "ID")
    ts(T.BI[:], T.cb[:], pp, BIG, eq, mul, "cb pf", "BI")
    tt(pf[:, 11:12], MK[:, 1:2], MK[:, 2:3], add, "MK", "pf11")
    ts(T.NI[:], T.cb[:], pp, -1.0, eq, mul, "cb pf", "NI")
    ts(T.Z[:, 432 + 15:432 + 143:16], ic[:, 0:8], pg, pf[:, 11:12], eq, mul, "ic pf pf11 Z", "Z3")
    ts(pf[:, 12:13], MK[:, 0:1], -0.5, pf[:, 11:12], mul, add, "MK pf11", "pf12")
    ts(T.D0[:], T.cm[:], 0.0, RV, eq, mul, "cm", "D0")
    ts(T.Z[:, 288 + 15:288 + 143:16], ic[:, 0:8], pg, pf[:, 12:13], eq, mul, "ic pf pf12 Z", "Z2")
    ts(T.ai2[0:64, :], T.ai[0:64, :], 31, None, an_, None, "aia", "a2a")
    ts(T.ai2[64:128, :], T.ai[64:128, :], 992, None, an_, None, "aib", "a2b")
    cp(T.thr[:, 1:2], T.wi0[:, 0:1], "wi0", "wf")
    cp(T.lh[:], T.ai2[:], "a2a a2b", "lh")
    ts(T.WB[:], T.BO[:], T.thr[:, 1:2], 2.0, mul, mul, "BO wf", "WB")
    ts(T.YL[:], T.iy[:, 0:NY], pf[:, 9:10], None, add, None, "iy pf9", "YL")
    ts(T.PL[:], ic[:, 0:8], 2.0, pf[:, 8:9], mul, add, "ic pf8", "PL")
    cp(TEAM, T.ti[:], "ti", "TW")

    late = [
        lambda: ts(T.Z[:, 144 + 15:144 + 143:16], ic[:, 0:8], pg, -65536.0, eq, mul, "ic pf Z", "Z1"),
        lambda: cp(T.BO32[:], T.BO[:], "BO", "BO32"),
        lambda: ts(T.lam[:], ic[:, 0:8], 16.0, pm, mul, add, "ic pf", "lam"),
        lambda: ts(T.DS[:], T.cm[:], 0.0, None, AL.not_equal, None, "cm", "DS"),
        lambda: ts(pf[:, 13:14], pf[:, 11:12], -1.0, 1.0, mul, add, "pf11", "pf13"),
        lambda: ts(pf[:, 14:15], MK[:, 1:2], 256.0, None, mul, None, "MK", "pf14"),
        lambda: ts(pf[:, 15:16], MK[:, 1:2], -256.0, None, mul, None, "MK", "pf15"),
        lambda: ts(T.thr[:, 2:3], MK[:, 2:3], 256.0, None, mul, None, "MK", "clb"),
        lambda: ts(T.thr[:, 3:4], pm, -1.0, None, mul, None, "pf", "npm"),
        lambda: ts(T.dum[:], T.lam[:], float(PN + NT), None, add, None, "lam", "dum"),
        lambda: ts(T.cdm[:], T.lam[:], -1.0, -float(NT), mul, add, "lam", "cdm"),
        lambda: ts(T.dumf[:], T.lam[:], 1.0 + 1.0 / 512, float(PN + NT), mul, add, "lam", "dumf"),
        lambda: cp(T.I32[:], T.ID[:], "ID", "I32"),
        lambda: ts(T.I12[:], T.ID[:], 12.0, None, mul, None, "ID", "I12"),
        lambda: ms(T.thr[:, 0:1], 0.0, "thr"),
        lambda: ts(s8[:, 96:97], pf[:, 3:4], 8.0, 24.0, mul, add, "pf", "w0"),
        lambda: ts(s8[:, 97:98], pf[:, 3:4], 2.5, 580.0, AL.is_lt, mul, "pf", "w1"),
        lambda: ts(s8[:, 99:100], pf[:, 3:4], 480.0, None, add, None, "pf", "w3"),
        lambda: ts(s8[:, 98:99], s8[:, 96:97], pf[:, 3:4], -81.0, mul, add, "w0 pf", "w2"),
        lambda: ts(T.wl[:, 0:1], s8[:, 98:99], s8[:, 97:98], s8[:, 99:100], add, AL.min, "w1 w2 w3", "wl"),
    ]

    def constants(k):
        for _ in range(k):
            if late:
                late.pop(0)()

    QB = [0, 1, 2, 4, 5, 6, 7, 3]

    def q_prog(c):
        mm(T["B%d" % QB[c]][:], Zw(0, 0), T.P[:, 512 * c:512 * c + 512], True, False, "Z0 P%d" % (c // 2), "B%d" % QB[c])

    def q_act(c):
        mm(T["B%d" % QB[c]][:], T.sel[:, 128 * c:128 * c + 128], T.lh[:], False, True, "sel%d lh" % c, "B%d" % QB[c])

    def q_copy(c, e):
        if e == "v":
            cp(T.Q[:, 512 * c:512 * c + 512], T["B%d" % QB[c]][:], "B%d" % QB[c], "Q%d" % c)
        else:
            act(T.Q[:, 512 * c:512 * c + 512], T["B%d" % QB[c]][:], AF.Copy, "B%d" % QB[c], "Q%d" % c)

    def spread(v, j):
        if early.get(v):
            return
        if j < 0:
            cp(T.Y4[:], T["X%d" % v][:, 0:128].indirect(T.YL[:]), "YL X%d" % v, "Y4")
        else:
            cp(T.XE[:, 128 * SA + j:2048:4], T.Y4[:], "Y4", ("XEb", "XEc", "XEd")[j - 1] if j else _names("XE", SA, 16))

    def begin(v):
        X, xn = T["X%d" % v], "X%d" % v
        x = X[:, 0:128]
        if v == 0:
            q_prog(0); q_prog(1)
        mm(E[:, 0:128], T.WB[:], x, True, True, "WB " + xn, "B3")
        for a0, a1 in [(0, 4), (4, SA)] + ([(SA, 16)] if early.get(v) else []):
            act(T.XE[:, 128 * a0:128 * a1], x.indirect(T.LS[:, 48 + 8 * a0:48 + 8 * a1]), AF.Copy, "LS " + xn, _names("XE", a0, a1))
        spread(v, -1)
        cp(T.e1[:], E[:, 0:128], "B3", "e1")
        if v == 0:
            cp(T.lst[:], T.sti[:], "sti", "lst")
        else:
            ts(T.lst[:], X[:, 128:136], 256.0, None, add, None, xn, "lst")
        ts(T.e2[:], T.e1[:], 511, None, an_, None, "e1", "e2")
        spread(v, 0)
        ts(T.E33[:], T.e2[:], 33.0, None, add, None, "e2", "E33")
        spread(v, 1)

    begin(0)
    for v in range(NV):
        X, xn, Gl, gn, O, on = T["X%d" % v], "X%d" % v, T["G%d" % v], "G%d" % v, T["O%d" % v], "O%d" % v
        x = X[:, 0:128]
        last = v == NV - 1
        for s in range(ST):
            nb, nn = (T.n0, "n0") if s == 0 else (T.n1, "n1")
            if s == 0:
                tt(T.m32[:], TEAM.indirect(T.lst[:]), T.E33[:], mul, "TW lst E33", "m32")
                spread(v, 2)
            else:
                tt(T.m32[:], TWIN.indirect(T.lst[:]), T.E33[:], mul, "TW TWz lst E33", "m32")
            ts(nb[:], T.m32[:], 5, 4095, sh, an_, "m32", nn)
            if s == 0:
                spread(v, 3)
            cp(T.n16[:], nb[:].indirect(T.PL[:]), "PL " + nn, "n16")
            if v == 0 and s == 0:
                q_prog(2); q_prog(3)
                for c in range(4):
                    q_act(c)
                for c in range(4, 8):
                    q_prog(c); q_act(c)
                for c, e in enumerate(QE):
                    q_copy(c, e)
            mm(K[:, 0:128], T.ID[:], T.KI[:], True, False, "ID KI", "B0")
            for a0, a1 in zip(CV, CV[1:]):
                cols = slice(128 * a0, 128 * a1)
                tt(T.M[:, cols], T.P[:].indirect(T.n16[:, 8 * a0:8 * a1]), T.XE[:, cols], AL.max,
                   PALL + " n16 " + _names("XE", a0, a1) + (" XEb XEc XEd" if a1 > SA else ""), _names("M", a0, a1))
            for a0, a1 in zip(CS, CS[1:]):
                act(T.G[:, 128 * a0:128 * a1], T.Q[:, 0:PN].indirect(T.n16[:, 8 * a0:8 * a1]), AF.Copy, QALL + " n16", _names("Ga", a0, a1))
            for k, a in _tensor_order():
                cols = slice(128 * a, 128 * a + 128)
                if k == 0:
                    mm(A[:, 0:128], Zw(3, a), T.G[:, cols], a == 0, a == 15, "Z3 Ga%d" % a, "B1")
                elif k == 1:
                    mm(K[:, 0:128], Zw(2, a), T.G[:, cols], False, False, "Z2 Ga%d" % a, "B0")
                else:
                    mm(K[:, 0:128], Zw(0, a), T.M[:, cols], False, False, "Z0 M%d" % a, "B0")
            if s == 0:
                if v == 0:
                    cp(T.TX[:, 0:128], T.sti[:].indirect(exl(5)), "sti LS", "TX0")
                    cp(H[:, 0:40:5], T.sti[:], "sti Hz", "H0")
                else:
                    act(T.TX[:, 0:128], X[:, 128:136].indirect(exl(5)), AF.Identity, xn + " LS", "TX0", bias=256.0)
                    ts(H[:, 0:40:5], X[:, 128:136], 256.0, None, add, None, xn, "H0")
                    red(T.cn[:, 0:1], S8(7), add, "s7", "cn")
            else:
                ts(T.dl[:], H[:, s:40:5], 512.0, RV, AL.is_lt, mul, "H%d" % s, "dl")
                constants(3)
            if v == 0 and s < 3:
                for a in range((0, 4, 10)[s], (4, 10, 16)[s]):
                    act(T.sa[:, 128 * a:128 * a + 128], T.BO[:], AF.Copy, "BO MK", "sa%d" % a, scale=MK[:, a:a + 1])
            if s == 1:
                ts(T.k0[:], WI[:, 0:40:5], 11, 15, sh, an_, "WI", "k0")
            if s == 2:
                ts(R1[:, 0:128], R1[:, 0:128], pm, None, eq, None, "B4 pf", "B4")
            if s == 3:
                tt(T.fm[:], R1[:, 128:256], MK[:], mul, "B4 MK", "fm")
            for j in range(s + 1):
                tt(T.EQ[:, 128 * j:128 * j + 128], A[:, 0:128], T.TX[:, 128 * j:128 * j + 128], eq, "B1 TX%d" % j, "EQ%d" % j)
                mm(K[:, 0:128], T.BI[:], T.EQ[:, 128 * j:128 * j + 128], False, j == s, "BI EQ%d" % j, "B0")
            if s == 0:
                mm(E[:, 0:128], T.NI[:], Gl[:], True, False, "NI " + gn, "B3")
                mm(E[:, 0:128], T.ID[:], x, False, True, "ID " + xn, "B3")
                act(T.uo[:], E[:, 0:128], AF.Abs, "B3", "uo")
                act(T.E97[:], T.E33[:], AF.Identity, "E33", "E97", bias=-1599.5, scale=48.5)
                if v:
                    mm(R2[:, 256:257], T.BO32[:], T.cn[:, 0:1], True, True, "BO32 cn", "B5")
                constants(5)
            else:
                if s == 1:
                    tt(T.k0x[:], T.k0[:].indirect(exl(5)), MK[:], mul, "k0 LS MK", "k0x")
                if s == 2:
                    tt(T.nf[:], R1[:, 0:128], T.n0[:], mul, "B4 n0", "nf")
                if s == 3:
                    scan(T.fs[:], T.DS[:], T.fm[:], mul, add, "DS fm", "fs")
                tt(T.D[:], T.dl[:], H[:, s:40:5], AL.max, "dl H%d" % s, "D")
                constants(2)
            if v and s == 2:
                ts(T.thr[:, 0:1], T.ac[:, 4:5], 65536.0, None, mul, None, "ac4", "thr")
            scan(T.W[:], T.D0[:], K[:, 0:128], AL.max, AL.min, "D0 B0", "W")
            if s == 1 and v == 1:
                cp(T.ac[:, 0:1], R2[:, 256:257], "B5", "ac0")
            if s == 1 and v == 2:
                tt(T.ac[:, 0:1], R2[:, 256:257], T.ac[:, 0:1], add, "B5 ac0", "ac0")
            if s == 3:
                tt(S8(0), T.fs[:, 15:128:16], T.dum[:], sub, "fs dum", "s0")
            if s == 0:
                cp(WI[:, 0:40:5], T.W[:, 15:128:16], "W WIz", "WI")
            else:
                tt(WI[:, s:40:5], T.W[:, 15:128:16], T.D[:], AL.min, "W D", "WI")
            if s == 1 and v:
                ts(T.ac[:, 4:5], T.ac[:, 0:1], 7, None, an_, None, "ac0", "ac4")
            if s == 3 and not last:
                cp(T.fl[:], T.fs[:, 15:128:16], "fs", "fl")
            ts(H[:, s + 1:40:5], WI[:, s:40:5], 2047, None, an_, None, "WI", "H%d" % (s + 1))
            if s == 3:
                ts(T.kk[:], WI[:], 11, 15, sh, an_, "WI", "kk")
            cp(T.lst[:], H[:, s + 1:40:5], "H%d" % (s + 1), "lst")
            if s < ST - 1:
                cp(T.hf[:, 8 * s:8 * s + 8], H[:, s + 1:40:5], "H%d" % (s + 1), "hf%d" % s)
                act(T.TX[:, 128 * s + 128:128 * s + 256], T.hf[:, 8 * s:8 * s + 8].indirect(exl(5)), AF.Copy, "hf%d LS" % s, "TX%d" % (s + 1))
            if s == 0:
                for a in range(16):
                    mm(GN[:, 0:8], Zw(0, a), T.uo[:, a:128:16], a == 0, False, "Z0 uo", "B2")
            if s == 1:
                mm(R1[:, 0:128], T.BO[:], T.k0x[:], True, True, "BO k0x", "B4")
                if last:
                    dma("g", T.AW[0:128:16, 0:PN], T.Q[1:128:16, 0:PN], QALL, "AW")
                    dma("g", T.AW[0:128:16, 0:PN], T.Q[2:128:16, 0:PN], QALL + " AW", "AW", accum_op=add, max_dma_last_dim=4096)
            if s == 2:
                mm(R1[:, 128:256], T.BO32[:], T.nf[:], True, True, "BO32 nf", "B4")
                mm(E[:, 0:128], T.NI[:], Gl[:], True, False, "NI " + gn, "B3")
        constants(99)
        HA = "H0 H1 H2 H3 H4"
        mm(A[:, 0:128], T.I32[:], T.E97[:], True, False, "I32 E97", "B1")
        ts(T.lt[:], H[:], 512.0, None, AL.is_lt, None, HA, "lt")
        tt(T.dx[:], T.EW[:].indirect(T.lst[:]), x, sub, "EWa EWb EWc lst " + xn, "dx")
        act(O[:, 0:128], T.dx[:], AF.Abs, "dx", on)
        if last:
            send(v + 1)
        tt(T.vv[:], H[:], T.lt[:], mul, HA + " lt", "vv")
        ts(T.ge[:], H[:], 512.0, None, AL.is_ge, None, HA, "ge")
        ts(T.a1[:], H[:], 1024.0, None, eq, None, HA, "a1")
        scan(CU[:], T.ge[:], T.vv[:], mul, add, "ge vv", "CU")
        tt(T.nv[:, 0:39], T.ge[:, 0:39], T.a1[:, 1:40], AL.max, "ge a1", "nv")
        ts(O[:, 128:136], CU[:, 4:40:5], -256.0, None, add, None, "CU", on + "c")
        if not last:
            send(v + 1)
        mm(E[:, 0:128], T.ID[:], O[:, 0:128], False, True, "ID " + on, "B3")
        act(T.un[:], E[:, 0:128], AF.Abs, "B3", "un")
        if not last:
            act(T.qk[:], T.Q[:, 0:PN].indirect(T.fl[:]), AF.Identity, QALL + " fl pf13 pf14", "qk", bias=pf[:, 14:15], scale=pf[:, 13:14])
        for a in range(16):
            mm(GN[:, 0:8], Zw(1, a), T.un[:, a:128:16], False, a == 15, "Z1 un", "B2")
        ts(T.va[:, 0:39], T.nv[:, 0:39], -1.0, 1.0, mul, add, "nv", "va")
        tt(T.vt[:, 0:39], T.va[:, 0:39], CU[:, 0:39], mul, "va CU", "vt")
        tt(T.vk[:, 0:39], T.va[:, 0:39], T.kk[:, 0:39], mul, "va kk", "vk")
        scan(T.LT[:, 0:39], T.nv[:, 0:39], T.vt[:, 0:39], mul, add, "nv vt", "LT")
        scan(T.LK[:, 0:39], T.nv[:, 0:39], T.vk[:, 0:39], mul, add, "nv vk", "LK")
        cp(T.tl[:], T.LT[:, 3:39:5], "LT", "tl")
        act(T.c1[:], TEAM.indirect(T.tl[:]), AF.Copy, "TW tl", "c1")
        cp(O[:, 136:144], T.LK[:, 3:39:5], "LK", "kca")
        for a in range(16):
            mm(R2[:, a:256:16], T.sa[:, 128 * a:128 * a + 128], O[:, 128:144], True, True, "sa%d kca %sc" % (a, on), "B5")
        mm(A[:, 0:128], T.I12[:], T.c1[:], False, True, "I12 c1", "B1")
        tt(S8(1), CU[:, 4:40:5], CU[:, 0:40:5], AL.not_equal, "CU", "s1")
        tt(S8(2), T.LT[:, 3:39:5], T.cdm[:], add, "LT cdm", "s2")
        tt(S8(3), S8(0), S8(1), mul, "s0 s1", "s3")
        tt(S8(4), S8(2), T.va[:, 0:39:5], mul, "s2 va", "s4")
        ts(S8(7), GN[:, 0:8], T.thr[:, 0:1], None, AL.is_gt, None, "B2 thr", "s7")
        tt(S8(5), S8(3), S8(4), sub, "s3 s4", "s5")
        tt(S8(6), S8(4), T.dumf[:], add, "s4 dumf", "s6")
        tt(S8(8), S8(7), S8(5), mul, "s7 s5", "s8")
        tt(S8(9), S8(8), S8(6), add, "s8 s6", "s9")
        tt(S8(10), S8(8), S8(4), add, "s8 s4", "s10")
        tt(T.kx[:], S8(9).indirect(exl(5)), MK[:], mul, "s9 LS MK", "kx")
        mm(V1[:, 0:128], T.BO32[:], T.kx[:], True, True, "BO32 kx", "B6")
        mm(V2[:, 0:48], T.BO32[:], T.kx[:, 0:48], True, True, "BO32 kx", "B7")
        ts(S8(11), S8(9), -1.0, 0.25, mul, add, "s9", "s11")
        act(T.u1[:], R2[:, 128:256], AF.Abs, "B5 npm", "u1", bias=T.thr[:, 3:4])
        act(T.u2[:], T.u1[:], AF.Relu, "u1", "u2", bias=1.0, scale=-1.0)
        for b in range(3, 8):
            act(T.db[:, DO[b]:DO[b + 1]], V1[:, 0:16 * b + 16], AF.Abs, "B6 s11", "df%d" % b, bias=s8[:, 88 + b:89 + b])
        if last:
            act(T.av[:], R2[:, 0:128], AF.Identity, "B5", "av", bias=256.0)
        else:
            ts(R2[:, 0:128], R2[:, 0:128], pf[:, 15:16], T.thr[:, 2:3], AL.max, AL.min, "B5 pf15 clb", "B5")
        tt(A[:, 0:128], A[:, 0:128], T.u2[:], mul, "B1 u2", "B1")
        for b in range(3):
            ts(T.df[:, 64 * b:64 * b + 16 * b + 16], V2[:, 0:16 * b + 16], s8[:, 88 + b:89 + b], None, add, None, "B7 s11", "df%d" % b)
        tt(T.t3[:], A[:, 0:128], T.c1[:], add, "B1 c1", "t3")
        if not last:
            tt(T.qv[:], R2[:, 0:128], T.qk[:], add, "B5 qk", "qv")
        for b in range(3):
            red(T.dm[:, 480 + b:481 + b], T.df[:, 64 * b:64 * b + 16 * b + 16], AL.min, "df%d" % b, "mn%d" % b, apply_absolute_value=True)
        ts(T.tv[:], T.t3[:], 4095, None, an_, None, "t3", "tv")
        if not last and early[v + 1]:
            begin(v + 1)
        scan(T.dm[:, 0:480], T.dr[:], T.db[:], AL.max, AL.min, "dr df3 df4 df5 df6 df7", "dm")
        ts(T.wr[:], T.dm[:, 0:483].indirect(T.wl[:, 0:1]), 0.25, None, AL.is_ge, None, "dm mn0 mn1 mn2 wl", "s13")
        tt(S8(14), T.wr[:, 0:8], S8(10), mul, "s13 s10", "s14")
        tt(S8(15), S8(14), T.dum[:], add, "s14 dum", "s15")
        cp(T.sl[:], S8(15), "s15", "sl")
        cp(T.TW[:, 0:KW].indirect(T.sl[:]), T.tv[:], "sl tv", "TW TWz")
        if last:
            dma("y", T.yteam[:], TEAM, "TW", "yteam")
            cp(T.AW[:].indirect(T.sl[:]), T.av[:], "sl av", "AW")
            dma("y", T.yact[:], T.AW[0:128:16, 0:PN], "AW", "yact")
        else:
            cp(T.Q[:].indirect(T.sl[:]), T.qv[:], "sl qv", QALL)
            if not early[v + 1]:
                begin(v + 1)
    dma("s", T.yx[:], T.XF[:], "XF", "yx")
    rec("g", "x", None, "yx yteam yact", "")
    _emit(ops, g, T)
    g.wait_ge(T.sem.ls, sent[0])
